import numpy as np
import ml_dtypes


def mxq(x, axis, fmt="e4m3"):
    dtype, down = {"e4m3": (ml_dtypes.float8_e4m3fn, 7), "e5m2": (ml_dtypes.float8_e5m2, 14)}[fmt]
    v = np.moveaxis(np.asarray(x, np.float32).astype(ml_dtypes.bfloat16).astype(np.float64), axis, -1)
    blocks = v.reshape(v.shape[:-1] + (-1, 32))
    amax = np.abs(blocks).max(-1, keepdims=True)
    byte = np.maximum(np.where(amax > 0, np.frexp(amax)[1] - 1 + 127, 0) - down, 1)
    scale = np.exp2(byte - 127.0)
    codes = (blocks / scale).astype(np.float32).astype(dtype).astype(np.float64)
    return np.moveaxis((codes * scale).reshape(v.shape), -1, axis)


WIDE = False


def mx_kscale(k):
    if not WIDE:
        return np.ones(k)
    levels = np.array([10, -10, 5, -5, 0])
    if k % 512:
        return np.exp2(np.random.permutation(np.resize(levels, k // 32))).repeat(32)
    a = np.empty((k // 512, 16))
    for p in range(k // 512):
        a[p, :8] = np.random.permutation(np.resize(levels, 8))
        for g in range(8):
            far = levels[np.abs(levels - a[p, g]) >= 10]
            a[p, g + 8] = far[np.random.randint(len(far))]
    return np.exp2(a.ravel()).repeat(32)


def f64(x):
    return np.asarray(x).astype(np.float64)


def striped(idx):
    return np.tile(idx.reshape(-1, 16).T, (8, 1)).astype(np.uint16)


def unstriped(offs):
    return offs[:16].T.reshape(-1).astype(np.int64)


def striped8(idx):
    return np.concatenate([x.reshape(-1, 16).T for x in idx]).astype(np.uint16)


def runs(offs, k):
    lists = np.stack([offs[16 * r : 16 * r + 16].T.reshape(-1) for r in range(8)]).astype(np.int64)
    return lists[np.arange(k) % 512 // 64]


def pack_weight(w):
    k, n = w.shape
    w = f64(np.asarray(w, np.float32).astype(ml_dtypes.bfloat16)).reshape(k // 32, 32, n)
    amax = np.abs(w).max(1)
    byte = np.clip(np.where(amax > 0, np.frexp(amax)[1] - 1 + 127 - 7, 1), 1, 254)
    scaled = (w * np.exp2(127.0 - byte)[:, None, :]).reshape(k, n).astype(np.float32)
    words = np.ascontiguousarray(scaled.reshape(k // 512, 128, 4, n).transpose(0, 1, 3, 2)).astype(ml_dtypes.float8_e4m3fn).view(np.uint8)
    return words, np.ascontiguousarray(byte.astype(np.uint8).reshape(k // 512, 16, n))


def unpack_weight(words, scales):
    g, p, n, _ = words.shape
    vals = np.ascontiguousarray(words).view(ml_dtypes.float8_e4m3fn).astype(np.float64) * np.repeat(np.exp2(scales.astype(np.float64) - 127.0), 8, axis=1)[..., None]
    return vals.transpose(0, 1, 3, 2).reshape(g * 512, n)

def planes(y):
    n, m = y.shape
    v = y.astype(np.float32).astype(ml_dtypes.bfloat16).astype(np.float64).reshape(n // 32, 32, m)
    top = np.abs(v).max(1)
    byte = np.clip(np.where(top > 0, np.frexp(top)[1] - 1 + 127 - 7, 1), 1, 254)
    codes = (v * np.exp2(127.0 - byte)[:, None, :]).reshape(n, m).astype(np.float32).astype(ml_dtypes.float8_e4m3fn).view(np.uint8)
    words = codes.reshape(n // 512, 128, 4, m).transpose(0, 1, 3, 2)
    return np.ascontiguousarray(words), np.ascontiguousarray(byte.astype(np.uint8).reshape(n // 512, 16, m))


K, T, S, N, H = 512, 2048, 512, 512, 512


def setup_inputs():
    n = np.random.standard_normal
    s = mx_kscale(K)[:, None]
    u = mx_kscale(S)
    packed_xT = pack_weight(n((K, T)) * s)
    packed_w1 = pack_weight(n((S, N)) / np.sqrt(S) / u[:, None])
    return {
        "x_words": packed_xT[0],
        "x_scales": packed_xT[1],
        "wa": (n((K, H)) / np.sqrt(K) / s).astype(np.float32),
        "gt": (np.random.uniform(0.5, 1.5, (S, 1)) * u[:, None]).astype(np.float32),
        "w1_words": packed_w1[0],
        "w1_scales": packed_w1[1],
        "offs": striped(np.random.permutation(T)[:S]),
        "fl": striped8(np.stack([np.random.permutation(H) for _ in range(8)])),
    }


def reference(x_words, x_scales, wa, gt, w1_words, w1_scales, offs, fl):
    xq = unpack_weight(x_words, x_scales)[:, unstriped(offs)]
    y = xq.T @ mxq(f64(wa), 0, "e4m3")
    pw = (y) ** 2
    z = f64(gt) * ((y[np.arange(S)[:, None], runs(fl, S)]) * ((2.0 * pw) / (pw + pw[np.arange(S)[:, None], runs(fl, S)] + 0.25)))
    out_0 = unpack_weight(w1_words, w1_scales).T @ mxq(z, 0, "e4m3")
    return (out_0,) + planes(out_0)

@@ -1,0 +1,226 @@
+from contextlib import ExitStack
+
+import concourse.mybir as mybir
+
+K, T, S, N, H = 512, 2048, 512, 512, 512
+FLOPS = 2 * K * S * H + 2 * S * N * H
+
+F32 = mybir.dt.float32
+BF16 = mybir.dt.bfloat16
+I32 = mybir.dt.int32
+U32 = mybir.dt.uint32
+U16 = mybir.dt.uint16
+U8 = mybir.dt.uint8
+FP8X4 = mybir.dt.float8_e4m3fn_x4
+ACT = mybir.ActivationFunctionType
+ALU = mybir.AluOpType
+
+P = 128
+PACK = 4
+HALF = H // 2
+CHUNKS = [(0, 256), (256, 128), (384, 128)]
+B_SCALAR = 128
+
+
+def words_view(dram):
+    return dram[0].rearrange("p n t -> p (n t)").bitcast(I32)
+
+
+def load_scale_rows(queue, tile, dram):
+    for q in range(4):
+        queue.dma_start(out=tile[32 * q : 32 * q + 4, :].bitcast(I32), in_=dram[0, 4 * q : 4 * q + 4, :].bitcast(I32))
+
+
+def deal(nc, dst, src, run):
+    nc.vector.tensor_copy(
+        out=dst.rearrange("p (t b i) -> p b t i", t=PACK, i=run),
+        in_=src.rearrange("p (b i t) -> p b t i", t=PACK, i=run),
+    )
+
+
+def woven(flat):
+    return flat.rearrange("p (c i t) -> p c t i", i=2, t=PACK)
+
+
+def planes(rows):
+    return rows.rearrange("p t (c i) -> p c t i", i=2)
+
+
+def tile_picked_featnorm_none_po_kernel(
+    tc, x_words, x_scales, wa, gt, w1_words, w1_scales, offs, fl, out_0, out_1, out_2
+):
+    nc = tc.nc
+    with ExitStack() as ctx:
+        lists = ctx.enter_context(tc.tile_pool(name="lists", bufs=1))
+        keep = ctx.enter_context(tc.tile_pool(name="keep", bufs=1))
+        psum = ctx.enter_context(tc.psum_pool(name="psum", bufs=1))
+
+        def sb(name, shape, dtype):
+            return keep.tile(shape, dtype, name=name, align_bytes=64)
+
+        offs_sb = lists.tile([P, S // 16], U16, name="offs_sb")
+        fl_sb = lists.tile([P, H // 16], U16, name="fl_sb")
+        xw = sb("xw", [P, T], I32)
+        xs = sb("xs", [P, T], U8)
+        w1w = sb("w1w", [P, N], I32)
+        w1s = sb("w1s", [P, N], U8)
+        gt_sb = sb("gt_sb", [P, PACK], F32)
+        wa_raw = [sb("wa_raw%d" % h, [P, PACK, HALF], F32) for h in range(2)]
+        warm = sb("warm", [P, 2], F32)
+
+        nc.vector.memset(xs[:].bitcast(I32), 0)
+        nc.gpsimd.memset(warm[:, 0:1], 1.0)
+        nc.gpsimd.memset(w1s[:].bitcast(I32), 0)
+        nc.scalar.activation(out=warm[:, 1:2], in_=warm[:, 0:1], func=ACT.Abs_reciprocal_sqrt)
+
+        wa_rows = wa.rearrange("(p j) w -> p j w", j=PACK)
+        nc.sync.dma_start(offs_sb[:], offs)
+        nc.sync.dma_start(out=wa_raw[0][:], in_=wa_rows[:, :, 0:HALF])
+        load_scale_rows(nc.sync, xs, x_scales)
+        nc.sync.dma_start(out=xw[:], in_=words_view(x_words))
+        nc.sync.dma_start(out=wa_raw[1][:], in_=wa_rows[:, :, HALF:H])
+        nc.sync.dma_start(fl_sb[:], fl)
+        nc.sync.dma_start(out=gt_sb[:], in_=gt.rearrange("(p t) o -> p (t o)", t=PACK))
+        nc.sync.dma_start(out=w1w[:], in_=words_view(w1_words))
+        load_scale_rows(nc.sync, w1s, w1_scales)
+
+        wa_bf = [sb("wa_bf%d" % h, [P, HALF * PACK], BF16) for h in range(2)]
+        wa_q = [sb("wa_q%d" % h, [P, HALF], U32) for h in range(2)]
+        wa_s = [sb("wa_s%d" % h, [P, HALF], U8) for h in range(2)]
+
+        def quantise(codes, scales, values):
+            nc.vector.quantize_mx(out=codes.bitcast(FP8X4), scales=scales, in_=values)
+
+        def product(bank, lhs_w, lhs_s, t, rhs_w, rhs_s):
+            cols = slice(t * P, (t + 1) * P)
+            nc.tensor.matmul_mx(
+                out=bank,
+                lhsT=lhs_w[:, cols].bitcast(FP8X4),
+                lhsT_scale=lhs_s[:, cols],
+                rhs=rhs_w.bitcast(FP8X4),
+                rhs_scale=rhs_s,
+                start=True,
+                stop=True,
+            )
+
+        nc.scalar.copy(out=woven(wa_bf[0][:]), in_=planes(wa_raw[0][:]))
+
+        ps = sb("ps", [P, S], U8)
+        ds = sb("ds", [P, S], U8)
+        pw_ = sb("pw_", [P, S], U32)
+        dw = sb("dw", [P, S], U32)
+        nc.vector.tensor_copy(ps[:], xs[:].indirect(offs_sb[:]))
+        deal(nc, ds[:], ps[:], 16)
+        quantise(wa_q[0][:], wa_s[0][:], wa_bf[0][:])
+        nc.vector.tensor_copy(pw_[:], xw[:].bitcast(U32).indirect(offs_sb[:]))
+        deal(nc, dw[:], pw_[:], 4)
+
+        nc.scalar.copy(out=woven(wa_bf[1][:, 0 : B_SCALAR * PACK]), in_=planes(wa_raw[1][:, :, 0:B_SCALAR]))
+        nc.vector.tensor_copy(out=woven(wa_bf[1][:, B_SCALAR * PACK :]), in_=planes(wa_raw[1][:, :, B_SCALAR:]))
+        quantise(wa_q[1][:], wa_s[1][:], wa_bf[1][:])
+
+        ybank = [[psum.tile([P, 2, HALF], F32, name="ybank%d%d" % (h, u)) for u in range(2)] for h in range(2)]
+        y = [sb("y%d" % t, [P, H], F32) for t in range(PACK)]
+        pw = [sb("pw%d" % h, [P, PACK, HALF], F32) for h in range(2)]
+        for h in range(2):
+            for t in range(PACK):
+                product(ybank[h][t // 2][:, t % 2, :], dw, ds, t, wa_q[h][:], wa_s[h][:])
+        for t in range(PACK):
+            nc.scalar.copy(out=y[t][:, 0:HALF], in_=ybank[0][t // 2][:, t % 2, :])
+        for t in range(PACK):
+            if t < 2:
+                nc.vector.tensor_copy(out=y[t][:, HALF:H], in_=ybank[1][t // 2][:, t % 2, :])
+            else:
+                nc.scalar.copy(out=y[t][:, HALF:H], in_=ybank[1][t // 2][:, t % 2, :])
+        for u in range(2):
+            nc.scalar.activation(out=pw[0][:, 2 * u : 2 * u + 2, :], in_=ybank[0][u][:], func=ACT.Square)
+
+        d1w = sb("d1w", [P, N], U32)
+        d1s = sb("d1s", [P, N], U8)
+        o_s = sb("o_s", [P, H], U8)
+        out_rows = out_0.rearrange("(p t) j -> p t j", t=PACK)
+        out_words = words_view(out_1)
+
+        n = len(CHUNKS)
+        g, g2, r, q, zb, zq, zs, obank, of, ob, oq = ([None] * n for k in range(11))
+
+        def pw_of(c):
+            c0, w = CHUNKS[c]
+            return pw[c0 // HALF][:, :, c0 % HALF : c0 % HALF + w]
+
+        def gather(c):
+            c0, w = CHUNKS[c]
+            g[c] = sb("g%d" % c, [P, PACK, w], F32)
+            for t in range(PACK):
+                nc.vector.tensor_copy(g[c][:, t, :], y[t][:].indirect(fl_sb[:, c0 // 16 : (c0 + w) // 16]))
+            g2[c] = sb("gg%d" % c, [P, PACK, w], F32)
+            nc.scalar.activation(out=g2[c][:], in_=g[c][:], func=ACT.Square)
+
+        def denominator(c):
+            c0, w = CHUNKS[c]
+            d = sb("d%d" % c, [P, PACK, w], F32)
+            nc.vector.scalar_tensor_tensor(out=d[:], in0=g2[c][:], scalar=0.25, in1=pw_of(c), op0=ALU.add, op1=ALU.add)
+            root = sb("root%d" % c, [P, PACK, w], F32)
+            nc.scalar.activation(out=root[:], in_=d[:], func=ACT.Abs_reciprocal_sqrt, scale=0.5)
+            r[c] = sb("r%d" % c, [P, PACK, w], F32)
+            nc.scalar.activation(out=r[c][:], in_=root[:], func=ACT.Square)
+
+        def share(c):
+            c0, w = CHUNKS[c]
+            q[c] = sb("q%d" % c, [P, PACK, w], F32)
+            for t in range(PACK):
+                nc.vector.scalar_tensor_tensor(
+                    out=q[c][:, t, :], in0=pw_of(c)[:, t, :], scalar=gt_sb[:, t : t + 1], in1=r[c][:, t, :], op0=ALU.mult, op1=ALU.mult
+                )
+
+        def make_z(c):
+            c0, w = CHUNKS[c]
+            zb[c] = sb("zb%d" % c, [P, w * PACK], BF16)
+            nc.vector.tensor_tensor(out=woven(zb[c][:]), in0=planes(q[c][:]), in1=planes(g[c][:]), op=ALU.mult)
+
+        def mix(c):
+            c0, w = CHUNKS[c]
+            zq[c] = sb("zq%d" % c, [P, w], U32)
+            zs[c] = sb("zs%d" % c, [P, w], U8)
+            quantise(zq[c][:], zs[c][:], zb[c][:])
+            per = 512 // w
+            of[c] = sb("of%d" % c, [P, PACK, w], F32)
+            for b in range(PACK // per):
+                bank = psum.tile([P, per, w], F32, name="obank%d_%d" % (c, b))
+                for i in range(per):
+                    product(bank[:, i, :], d1w, d1s, b * per + i, zq[c][:], zs[c][:])
+                nc.scalar.copy(out=of[c][:, b * per : (b + 1) * per, :], in_=bank[:])
+            nc.sync.dma_start(out=out_rows[:, :, c0 : c0 + w], in_=of[c][:])
+
+        def round_out(c):
+            c0, w = CHUNKS[c]
+            ob[c] = sb("ob%d" % c, [P, w * PACK], BF16)
+            nc.vector.tensor_copy(out=woven(ob[c][:]), in_=planes(of[c][:]))
+
+        def planes_out(c):
+            c0, w = CHUNKS[c]
+            oq[c] = sb("oq%d" % c, [P, w], U32)
+            quantise(oq[c][:], o_s[:, c0 : c0 + w], ob[c][:])
+            nc.sync.dma_start(out=out_words[:, c0 : c0 + w], in_=oq[c][:].bitcast(I32))
+
+        def second_powers():
+            for u in range(2):
+                nc.scalar.activation(out=pw[1][:, 2 * u : 2 * u + 2, :], in_=ybank[1][u][:], func=ACT.Square)
+
+        def deal_w1():
+            deal(nc, d1w[:], w1w[:].bitcast(U32), 4)
+            deal(nc, d1s[:], w1s[:], 16)
+
+        stages = [gather, denominator, share, make_z, mix, round_out, planes_out]
+        deal_w1()
+        for step in range(n + len(stages) - 1):
+            for s in reversed(range(len(stages))):
+                c = step - s
+                if 0 <= c < n:
+                    stages[s](c)
+            if step == 0:
+                second_powers()
+
+        for qd in range(4):
+            queue = nc.sync if qd % 2 == 0 else nc.scalar
+            queue.dma_start(out=out_2[0, 4 * qd : 4 * qd + 4, :].bitcast(I32), in_=o_s[32 * qd : 32 * qd + 4, :].bitcast(I32))

@@ -18,8 +18,9 @@ ALU = mybir.AluOpType
 P = 128
 PACK = 4
 HALF = H // 2
-CHUNKS = [(0, 256), (256, 128), (384, 128)]
-B_SCALAR = 128
+W = 128
+CHUNKS = H // W
+ROUND_ON_SCALAR = 2
 
 
 def words_view(dram):
@@ -27,8 +28,8 @@ def words_view(dram):
 
 
 def load_scale_rows(queue, tile, dram):
-    for q in range(4):
-        queue.dma_start(out=tile[32 * q : 32 * q + 4, :].bitcast(I32), in_=dram[0, 4 * q : 4 * q + 4, :].bitcast(I32))
+    for r in range(4):
+        queue.dma_start(out=tile[r:P:32, :].bitcast(I32), in_=dram[0, r:16:4, :].bitcast(I32))
 
 
 def deal(nc, dst, src, run):
@@ -55,8 +56,8 @@ def tile_picked_featnorm_none_po_kernel(
         keep = ctx.enter_context(tc.tile_pool(name="keep", bufs=1))
         psum = ctx.enter_context(tc.psum_pool(name="psum", bufs=1))
 
-        def sb(name, shape, dtype):
-            return keep.tile(shape, dtype, name=name, align_bytes=64)
+        def sb(name, shape, dtype, tag=None):
+            return keep.tile(shape, dtype, name=name, tag=tag or name, align_bytes=64)
 
         offs_sb = lists.tile([P, S // 16], U16, name="offs_sb")
         fl_sb = lists.tile([P, H // 16], U16, name="fl_sb")
@@ -84,9 +85,6 @@ def tile_picked_featnorm_none_po_kernel(
         nc.sync.dma_start(out=w1w[:], in_=words_view(w1_words))
         load_scale_rows(nc.sync, w1s, w1_scales)
 
-        wa_bf = [sb("wa_bf%d" % h, [P, HALF * PACK], BF16) for h in range(2)]
-        wa_q = [sb("wa_q%d" % h, [P, HALF], U32) for h in range(2)]
-        wa_s = [sb("wa_s%d" % h, [P, HALF], U8) for h in range(2)]
 
         def quantise(codes, scales, values):
             nc.vector.quantize_mx(out=codes.bitcast(FP8X4), scales=scales, in_=values)
@@ -103,124 +101,139 @@ def tile_picked_featnorm_none_po_kernel(
                 stop=True,
             )
 
-        nc.scalar.copy(out=woven(wa_bf[0][:]), in_=planes(wa_raw[0][:]))
+        bf_a = sb("bf_a", [P, HALF * PACK], BF16)
+        nc.scalar.copy(out=woven(bf_a[:]), in_=planes(wa_raw[0][:]))
 
         ps = sb("ps", [P, S], U8)
         ds = sb("ds", [P, S], U8)
-        pw_ = sb("pw_", [P, S], U32)
-        dw = sb("dw", [P, S], U32)
         nc.vector.tensor_copy(ps[:], xs[:].indirect(offs_sb[:]))
         deal(nc, ds[:], ps[:], 16)
-        quantise(wa_q[0][:], wa_s[0][:], wa_bf[0][:])
-        nc.vector.tensor_copy(pw_[:], xw[:].bitcast(U32).indirect(offs_sb[:]))
-        deal(nc, dw[:], pw_[:], 4)
+        wa_q = [sb("wa_q%d" % h, [P, HALF], U32) for h in range(2)]
+        wa_s = [sb("wa_s%d" % h, [P, HALF], U8, "xs" if h == 0 else None) for h in range(2)]
+        quantise(wa_q[0][:], wa_s[0][:], bf_a[:])
+        dw = sb("dw", [P, S], U32, "ps")
+        nc.vector.tensor_copy(dw[:].rearrange("p (t m) -> p m t", t=PACK), xw[:].bitcast(U32).indirect(offs_sb[:]))
 
-        nc.scalar.copy(out=woven(wa_bf[1][:, 0 : B_SCALAR * PACK]), in_=planes(wa_raw[1][:, :, 0:B_SCALAR]))
-        nc.vector.tensor_copy(out=woven(wa_bf[1][:, B_SCALAR * PACK :]), in_=planes(wa_raw[1][:, :, B_SCALAR:]))
-        quantise(wa_q[1][:], wa_s[1][:], wa_bf[1][:])
+        bf_v = sb("bf_v", [P, W * PACK], BF16)
+        bf_s = sb("bf_s", [P, W * PACK], BF16)
+        nc.vector.tensor_copy(out=woven(bf_v[:]), in_=planes(wa_raw[1][:, :, 0:W]))
+        nc.vector.tensor_copy(out=woven(bf_s[:]), in_=planes(wa_raw[1][:, :, W:HALF]))
+        quantise(wa_q[1][:, 0:W], wa_s[1][:, 0:W], bf_v[:])
+        quantise(wa_q[1][:, W:HALF], wa_s[1][:, W:HALF], bf_s[:])
 
-        ybank = [[psum.tile([P, 2, HALF], F32, name="ybank%d%d" % (h, u)) for u in range(2)] for h in range(2)]
+        d1w = sb("d1w", [P, N], U32, tag="bf_s")
+        d1s = sb("d1s", [P, N], U8, tag="bf_v")
+
+        abank = [psum.tile([P, 2, HALF], F32, name="abank%d" % u, tag="abank%d" % u) for u in range(2)]
+        bbank = [psum.tile([P, HALF], F32, name="bbank%d" % t) for t in range(PACK)]
         y = [sb("y%d" % t, [P, H], F32) for t in range(PACK)]
-        pw = [sb("pw%d" % h, [P, PACK, HALF], F32) for h in range(2)]
-        for h in range(2):
-            for t in range(PACK):
-                product(ybank[h][t // 2][:, t % 2, :], dw, ds, t, wa_q[h][:], wa_s[h][:])
         for t in range(PACK):
-            nc.scalar.copy(out=y[t][:, 0:HALF], in_=ybank[0][t // 2][:, t % 2, :])
+            product(abank[t // 2][:, t % 2, :], dw, ds, t, wa_q[0][:], wa_s[0][:])
         for t in range(PACK):
-            if t < 2:
-                nc.vector.tensor_copy(out=y[t][:, HALF:H], in_=ybank[1][t // 2][:, t % 2, :])
-            else:
-                nc.scalar.copy(out=y[t][:, HALF:H], in_=ybank[1][t // 2][:, t % 2, :])
-        for u in range(2):
-            nc.scalar.activation(out=pw[0][:, 2 * u : 2 * u + 2, :], in_=ybank[0][u][:], func=ACT.Square)
+            product(bbank[t][:], dw, ds, t, wa_q[1][:], wa_s[1][:])
+        for t in range(PACK):
+            nc.scalar.copy(out=y[t][:, 0:HALF], in_=abank[t // 2][:, t % 2, :])
+        nc.vector.tensor_copy(out=y[0][:, HALF:H], in_=bbank[0][:])
+        for t in range(1, PACK):
+            nc.scalar.copy(out=y[t][:, HALF:H], in_=bbank[t][:])
+        deal(nc, d1w[:], w1w[:].bitcast(U32), 4)
+        deal(nc, d1s[:], w1s[:], 16)
 
-        d1w = sb("d1w", [P, N], U32)
-        d1s = sb("d1s", [P, N], U8)
         o_s = sb("o_s", [P, H], U8)
         out_rows = out_0.rearrange("(p t) j -> p t j", t=PACK)
         out_words = words_view(out_1)
+        n = CHUNKS
+        pw, g, gg, root, r, q, zb, obank, of, ob = ({} for k in range(10))
 
-        n = len(CHUNKS)
-        g, g2, r, q, zb, zq, zs, obank, of, ob, oq = ([None] * n for k in range(11))
+        def chunk(name, c, tag=None):
+            return sb("%s%d" % (name, c), [P, PACK, W], F32, tag)
 
-        def pw_of(c):
-            c0, w = CHUNKS[c]
-            return pw[c0 // HALF][:, :, c0 % HALF : c0 % HALF + w]
+        def power(c):
+            pw[c] = chunk("pw", c, ("wa_q1", "wa_s1")[c] if c < 2 else None)
+            cols = slice(c * W % HALF, c * W % HALF + W)
+            if c * W < HALF:
+                for u in range(2):
+                    nc.scalar.activation(out=pw[c][:, 2 * u : 2 * u + 2, :], in_=abank[u][:, :, cols], func=ACT.Square)
+            else:
+                for t in range(PACK):
+                    nc.scalar.activation(out=pw[c][:, t, :], in_=bbank[t][:, cols], func=ACT.Square)
 
         def gather(c):
-            c0, w = CHUNKS[c]
-            g[c] = sb("g%d" % c, [P, PACK, w], F32)
+            g[c] = chunk("g", c, "gg%d" % (c - 2) if c >= 2 else (None, "w1w")[c])
             for t in range(PACK):
-                nc.vector.tensor_copy(g[c][:, t, :], y[t][:].indirect(fl_sb[:, c0 // 16 : (c0 + w) // 16]))
-            g2[c] = sb("gg%d" % c, [P, PACK, w], F32)
-            nc.scalar.activation(out=g2[c][:], in_=g[c][:], func=ACT.Square)
+                nc.vector.tensor_copy(g[c][:, t, :], y[t][:].indirect(fl_sb[:, c * W // 16 : (c + 1) * W // 16]))
+
+        def square(c):
+            gg[c] = chunk("gg", c, "root%d" % (c - 2) if c >= 2 else None)
+            nc.scalar.activation(out=gg[c][:], in_=g[c][:], func=ACT.Square)
 
         def denominator(c):
-            c0, w = CHUNKS[c]
-            d = sb("d%d" % c, [P, PACK, w], F32)
-            nc.vector.scalar_tensor_tensor(out=d[:], in0=g2[c][:], scalar=0.25, in1=pw_of(c), op0=ALU.add, op1=ALU.add)
-            root = sb("root%d" % c, [P, PACK, w], F32)
-            nc.scalar.activation(out=root[:], in_=d[:], func=ACT.Abs_reciprocal_sqrt, scale=0.5)
-            r[c] = sb("r%d" % c, [P, PACK, w], F32)
-            nc.scalar.activation(out=r[c][:], in_=root[:], func=ACT.Square)
+            d = chunk("d", c)
+            nc.vector.scalar_tensor_tensor(out=d[:], in0=gg[c][:], scalar=0.25, in1=pw[c][:], op0=ALU.add, op1=ALU.add)
+            root[c] = chunk("root", c)
+            nc.scalar.activation(out=root[c][:], in_=d[:], func=ACT.Abs_reciprocal_sqrt, scale=0.5)
+
+        def inverse(c):
+            r[c] = chunk("r", c)
+            nc.scalar.activation(out=r[c][:], in_=root[c][:], func=ACT.Square)
 
         def share(c):
-            c0, w = CHUNKS[c]
-            q[c] = sb("q%d" % c, [P, PACK, w], F32)
+            q[c] = chunk("q", c)
             for t in range(PACK):
                 nc.vector.scalar_tensor_tensor(
-                    out=q[c][:, t, :], in0=pw_of(c)[:, t, :], scalar=gt_sb[:, t : t + 1], in1=r[c][:, t, :], op0=ALU.mult, op1=ALU.mult
+                    out=q[c][:, t, :], in0=pw[c][:, t, :], scalar=gt_sb[:, t : t + 1], in1=r[c][:, t, :], op0=ALU.mult, op1=ALU.mult
                 )
 
         def make_z(c):
-            c0, w = CHUNKS[c]
-            zb[c] = sb("zb%d" % c, [P, w * PACK], BF16)
+            zb[c] = sb("zb%d" % c, [P, W * PACK], BF16)
             nc.vector.tensor_tensor(out=woven(zb[c][:]), in0=planes(q[c][:]), in1=planes(g[c][:]), op=ALU.mult)
 
         def mix(c):
-            c0, w = CHUNKS[c]
-            zq[c] = sb("zq%d" % c, [P, w], U32)
-            zs[c] = sb("zs%d" % c, [P, w], U8)
-            quantise(zq[c][:], zs[c][:], zb[c][:])
-            per = 512 // w
-            of[c] = sb("of%d" % c, [P, PACK, w], F32)
-            for b in range(PACK // per):
-                bank = psum.tile([P, per, w], F32, name="obank%d_%d" % (c, b))
-                for i in range(per):
-                    product(bank[:, i, :], d1w, d1s, b * per + i, zq[c][:], zs[c][:])
-                nc.scalar.copy(out=of[c][:, b * per : (b + 1) * per, :], in_=bank[:])
-            nc.sync.dma_start(out=out_rows[:, :, c0 : c0 + w], in_=of[c][:])
+            zq = sb("zq%d" % c, [P, W], U32)
+            zs = sb("zs%d" % c, [P, W], U8)
+            quantise(zq[:], zs[:], zb[c][:])
+            obank[c] = psum.tile([P, PACK, W], F32, name="obank%d" % c, tag="obank%d" % c if c < 2 else "abank%d" % (c - 2))
+            for t in range(PACK):
+                product(obank[c][:, t, :], d1w, d1s, t, zq[:], zs[:])
 
-        def round_out(c):
-            c0, w = CHUNKS[c]
-            ob[c] = sb("ob%d" % c, [P, w * PACK], BF16)
-            nc.vector.tensor_copy(out=woven(ob[c][:]), in_=planes(of[c][:]))
+        def hand_out(c):
+            cols = slice(c * W, (c + 1) * W)
+            ob[c] = sb("ob%d" % c, [P, W * PACK], BF16, "d%d" % (n - 1) if c == 0 else None)
+            of[c] = chunk("of", c, "root%d" % (n - 1) if c == 0 else None)
+            if c < ROUND_ON_SCALAR:
+                nc.scalar.copy(out=woven(ob[c][:]), in_=planes(obank[c][:]))
+            nc.scalar.copy(out=of[c][:], in_=obank[c][:])
+            nc.sync.dma_start(out=out_rows[:, :, cols], in_=of[c][:])
+            if c >= ROUND_ON_SCALAR:
+                nc.vector.tensor_copy(out=woven(ob[c][:]), in_=planes(of[c][:]))
+            oq = sb("oq%d" % c, [P, W], U32)
+            quantise(oq[:], o_s[:, cols], ob[c][:])
+            nc.sync.dma_start(out=out_words[:, cols], in_=oq[:].bitcast(I32))
 
-        def planes_out(c):
-            c0, w = CHUNKS[c]
-            oq[c] = sb("oq%d" % c, [P, w], U32)
-            quantise(oq[c][:], o_s[:, c0 : c0 + w], ob[c][:])
-            nc.sync.dma_start(out=out_words[:, c0 : c0 + w], in_=oq[c][:].bitcast(I32))
+        for c in range(2):
+            power(c)
+            gather(c)
+            square(c)
+        for s in range(n + 2):
+            if s < n:
+                denominator(s)
+            if 2 <= s + 1 < n:
+                square(s + 1)
+            if s + 2 < n:
+                power(s + 2)
+            if s < n:
+                inverse(s)
+            if 0 <= s - 2:
+                make_z(s - 2)
+            if s + 2 < n:
+                gather(s + 2)
+            if 0 <= s - 1 < n:
+                share(s - 1)
+            if 0 <= s - 2:
+                mix(s - 2)
+        for c in range(n):
+            hand_out(c)
 
-        def second_powers():
-            for u in range(2):
-                nc.scalar.activation(out=pw[1][:, 2 * u : 2 * u + 2, :], in_=ybank[1][u][:], func=ACT.Square)
-
-        def deal_w1():
-            deal(nc, d1w[:], w1w[:].bitcast(U32), 4)
-            deal(nc, d1s[:], w1s[:], 16)
-
-        stages = [gather, denominator, share, make_z, mix, round_out, planes_out]
-        deal_w1()
-        for step in range(n + len(stages) - 1):
-            for s in reversed(range(len(stages))):
-                c = step - s
-                if 0 <= c < n:
-                    stages[s](c)
-            if step == 0:
-                second_powers()
-
-        for qd in range(4):
-            queue = nc.sync if qd % 2 == 0 else nc.scalar
-            queue.dma_start(out=out_2[0, 4 * qd : 4 * qd + 4, :].bitcast(I32), in_=o_s[32 * qd : 32 * qd + 4, :].bitcast(I32))
+        for row in range(4):
+            queue = nc.sync if row % 2 == 0 else nc.scalar
+            queue.dma_start(out=out_2[0, row:16:4, :].bitcast(I32), in_=o_s[row:P:32, :].bitcast(I32))

@@ -125,7 +125,7 @@ def tile_picked_featnorm_none_po_kernel(
         d1s = sb("d1s", [P, N], U8, tag="bf_v")
 
         abank = [psum.tile([P, 2, HALF], F32, name="abank%d" % u, tag="abank%d" % u) for u in range(2)]
-        bbank = [psum.tile([P, HALF], F32, name="bbank%d" % t) for t in range(PACK)]
+        bbank = [psum.tile([P, HALF], F32, name="bbank%d" % t, tag="bbank%d" % t) for t in range(PACK)]
         y = [sb("y%d" % t, [P, H], F32) for t in range(PACK)]
         for t in range(PACK):
             product(abank[t // 2][:, t % 2, :], dw, ds, t, wa_q[0][:], wa_s[0][:])
@@ -140,9 +140,11 @@ def tile_picked_featnorm_none_po_kernel(
         deal(nc, d1s[:], w1s[:], 16)
 
         o_s = sb("o_s", [P, H], U8)
+        o_q = sb("o_q", [P, H], U32)
         out_rows = out_0.rearrange("(p t) j -> p t j", t=PACK)
         out_words = words_view(out_1)
         n = CHUNKS
+        bank_tags = ["obank0", "obank1", "abank0", "abank1"] + ["bbank%d" % t for t in range(PACK)]
         pw, g, gg, root, r, q, zb, obank, of, ob = ({} for k in range(10))
 
         def chunk(name, c, tag=None):
@@ -192,23 +194,24 @@ def tile_picked_featnorm_none_po_kernel(
             zq = sb("zq%d" % c, [P, W], U32)
             zs = sb("zs%d" % c, [P, W], U8)
             quantise(zq[:], zs[:], zb[c][:])
-            obank[c] = psum.tile([P, PACK, W], F32, name="obank%d" % c, tag="obank%d" % c if c < 2 else "abank%d" % (c - 2))
+            obank[c] = [psum.tile([P, 2, W], F32, name="obank%d%d" % (c, u), tag=bank_tags[2 * c + u]) for u in range(2)]
             for t in range(PACK):
-                product(obank[c][:, t, :], d1w, d1s, t, zq[:], zs[:])
+                product(obank[c][t // 2][:, t % 2, :], d1w, d1s, t, zq[:], zs[:])
 
         def hand_out(c):
             cols = slice(c * W, (c + 1) * W)
-            ob[c] = sb("ob%d" % c, [P, W * PACK], BF16, "d%d" % (n - 1) if c == 0 else None)
-            of[c] = chunk("of", c, "root%d" % (n - 1) if c == 0 else None)
+            ob[c] = sb("ob%d" % c, [P, W * PACK], BF16)
+            for u in range(2):
+                nc.scalar.copy(out=of[c][:, 2 * u : 2 * u + 2, :], in_=obank[c][u][:])
+            nc.sync.dma_start(out=out_rows[:, :, cols], in_=of[c])
             if c < ROUND_ON_SCALAR:
-                nc.scalar.copy(out=woven(ob[c][:]), in_=planes(obank[c][:]))
-            nc.scalar.copy(out=of[c][:], in_=obank[c][:])
-            nc.sync.dma_start(out=out_rows[:, :, cols], in_=of[c][:])
-            if c >= ROUND_ON_SCALAR:
-                nc.vector.tensor_copy(out=woven(ob[c][:]), in_=planes(of[c][:]))
-            oq = sb("oq%d" % c, [P, W], U32)
-            quantise(oq[:], o_s[:, cols], ob[c][:])
-            nc.sync.dma_start(out=out_words[:, cols], in_=oq[:].bitcast(I32))
+                nc.scalar.copy(out=woven(ob[c][:]), in_=planes(of[c]))
+            else:
+                nc.vector.tensor_copy(out=woven(ob[c][:]), in_=planes(of[c]))
+            quantise(o_q[:, cols], o_s[:, cols], ob[c][:])
+            if c >= n - 2:
+                done = slice(0 if c == n - 2 else c * W, (c + 1) * W)
+                nc.sync.dma_start(out=out_words[:, done], in_=o_q[:, done].bitcast(I32))
 
         for c in range(2):
             power(c)
@@ -231,7 +234,9 @@ def tile_picked_featnorm_none_po_kernel(
                 share(s - 1)
             if 0 <= s - 2:
                 mix(s - 2)
+        early = sb("of_early", [P, 2, PACK, W], F32, "root%d" % (n - 1))
         for c in range(n):
+            of[c] = early[:, c, :, :] if c < 2 else chunk("of", c)[:]
             hand_out(c)
 
         for row in range(4):

from contextlib import ExitStack

import concourse.mybir as mybir

K, T, S, N, H = 512, 2048, 512, 512, 512
FLOPS = 2 * K * S * H + 2 * S * N * H

F32 = mybir.dt.float32
BF16 = mybir.dt.bfloat16
I32 = mybir.dt.int32
U32 = mybir.dt.uint32
U16 = mybir.dt.uint16
U8 = mybir.dt.uint8
FP8X4 = mybir.dt.float8_e4m3fn_x4
ACT = mybir.ActivationFunctionType
ALU = mybir.AluOpType

P = 128
PACK = 4
HALF = H // 2
W = 128
CHUNKS = H // W
ROUND_ON_SCALAR = 2


def words_view(dram):
    return dram[0].rearrange("p n t -> p (n t)").bitcast(I32)


def load_scale_rows(queue, tile, dram):
    for r in range(4):
        queue.dma_start(out=tile[r:P:32, :].bitcast(I32), in_=dram[0, r:16:4, :].bitcast(I32))


def deal(nc, dst, src, run):
    nc.vector.tensor_copy(
        out=dst.rearrange("p (t b i) -> p b t i", t=PACK, i=run),
        in_=src.rearrange("p (b i t) -> p b t i", t=PACK, i=run),
    )


def woven(flat):
    return flat.rearrange("p (c i t) -> p c t i", i=2, t=PACK)


def planes(rows):
    return rows.rearrange("p t (c i) -> p c t i", i=2)


def tile_picked_featnorm_none_po_kernel(
    tc, x_words, x_scales, wa, gt, w1_words, w1_scales, offs, fl, out_0, out_1, out_2
):
    nc = tc.nc
    with ExitStack() as ctx:
        lists = ctx.enter_context(tc.tile_pool(name="lists", bufs=1))
        keep = ctx.enter_context(tc.tile_pool(name="keep", bufs=1))
        psum = ctx.enter_context(tc.psum_pool(name="psum", bufs=1))

        def sb(name, shape, dtype, tag=None):
            return keep.tile(shape, dtype, name=name, tag=tag or name, align_bytes=64)

        offs_sb = lists.tile([P, S // 16], U16, name="offs_sb")
        fl_sb = lists.tile([P, H // 16], U16, name="fl_sb")
        xw = sb("xw", [P, T], I32)
        xs = sb("xs", [P, T], U8)
        w1w = sb("w1w", [P, N], I32)
        w1s = sb("w1s", [P, N], U8)
        gt_sb = sb("gt_sb", [P, PACK], F32)
        wa_raw = [sb("wa_raw%d" % h, [P, PACK, HALF], F32) for h in range(2)]
        warm = sb("warm", [P, 2], F32)

        nc.vector.memset(xs[:].bitcast(I32), 0)
        nc.gpsimd.memset(warm[:, 0:1], 1.0)
        nc.gpsimd.memset(w1s[:].bitcast(I32), 0)
        nc.scalar.activation(out=warm[:, 1:2], in_=warm[:, 0:1], func=ACT.Abs_reciprocal_sqrt)

        wa_rows = wa.rearrange("(p j) w -> p j w", j=PACK)
        nc.sync.dma_start(offs_sb[:], offs)
        nc.sync.dma_start(out=wa_raw[0][:], in_=wa_rows[:, :, 0:HALF])
        load_scale_rows(nc.sync, xs, x_scales)
        nc.sync.dma_start(out=xw[:], in_=words_view(x_words))
        nc.sync.dma_start(out=wa_raw[1][:], in_=wa_rows[:, :, HALF:H])
        nc.sync.dma_start(fl_sb[:], fl)
        nc.sync.dma_start(out=gt_sb[:], in_=gt.rearrange("(p t) o -> p (t o)", t=PACK))
        nc.sync.dma_start(out=w1w[:], in_=words_view(w1_words))
        load_scale_rows(nc.sync, w1s, w1_scales)


        def quantise(codes, scales, values):
            nc.vector.quantize_mx(out=codes.bitcast(FP8X4), scales=scales, in_=values)

        def product(bank, lhs_w, lhs_s, t, rhs_w, rhs_s):
            cols = slice(t * P, (t + 1) * P)
            nc.tensor.matmul_mx(
                out=bank,
                lhsT=lhs_w[:, cols].bitcast(FP8X4),
                lhsT_scale=lhs_s[:, cols],
                rhs=rhs_w.bitcast(FP8X4),
                rhs_scale=rhs_s,
                start=True,
                stop=True,
            )

        bf_a = sb("bf_a", [P, HALF * PACK], BF16)
        nc.scalar.copy(out=woven(bf_a[:]), in_=planes(wa_raw[0][:]))

        ps = sb("ps", [P, S], U8)
        ds = sb("ds", [P, S], U8)
        nc.vector.tensor_copy(ps[:], xs[:].indirect(offs_sb[:]))
        deal(nc, ds[:], ps[:], 16)
        wa_q = [sb("wa_q%d" % h, [P, HALF], U32) for h in range(2)]
        wa_s = [sb("wa_s%d" % h, [P, HALF], U8, "xs" if h == 0 else None) for h in range(2)]
        quantise(wa_q[0][:], wa_s[0][:], bf_a[:])
        dw = sb("dw", [P, S], U32, "ps")
        nc.vector.tensor_copy(dw[:].rearrange("p (t m) -> p m t", t=PACK), xw[:].bitcast(U32).indirect(offs_sb[:]))

        bf_v = sb("bf_v", [P, W * PACK], BF16)
        bf_s = sb("bf_s", [P, W * PACK], BF16)
        nc.vector.tensor_copy(out=woven(bf_v[:]), in_=planes(wa_raw[1][:, :, 0:W]))
        nc.vector.tensor_copy(out=woven(bf_s[:]), in_=planes(wa_raw[1][:, :, W:HALF]))
        quantise(wa_q[1][:, 0:W], wa_s[1][:, 0:W], bf_v[:])
        quantise(wa_q[1][:, W:HALF], wa_s[1][:, W:HALF], bf_s[:])

        d1w = sb("d1w", [P, N], U32, tag="bf_s")
        d1s = sb("d1s", [P, N], U8, tag="bf_v")

        abank = [psum.tile([P, 2, HALF], F32, name="abank%d" % u, tag="abank%d" % u) for u in range(2)]
        bbank = [psum.tile([P, HALF], F32, name="bbank%d" % t, tag="bbank%d" % t) for t in range(PACK)]
        y = [sb("y%d" % t, [P, H], F32) for t in range(PACK)]
        for t in range(PACK):
            product(abank[t // 2][:, t % 2, :], dw, ds, t, wa_q[0][:], wa_s[0][:])
        for t in range(PACK):
            product(bbank[t][:], dw, ds, t, wa_q[1][:], wa_s[1][:])
        for t in range(PACK):
            nc.scalar.copy(out=y[t][:, 0:HALF], in_=abank[t // 2][:, t % 2, :])
        nc.vector.tensor_copy(out=y[0][:, HALF:H], in_=bbank[0][:])
        for t in range(1, PACK):
            nc.scalar.copy(out=y[t][:, HALF:H], in_=bbank[t][:])
        deal(nc, d1w[:], w1w[:].bitcast(U32), 4)
        deal(nc, d1s[:], w1s[:], 16)

        o_s = sb("o_s", [P, H], U8)
        o_q = sb("o_q", [P, H], U32)
        out_rows = out_0.rearrange("(p t) j -> p t j", t=PACK)
        out_words = words_view(out_1)
        n = CHUNKS
        bank_tags = ["obank0", "obank1", "abank0", "abank1"] + ["bbank%d" % t for t in range(PACK)]
        pw, g, gg, root, r, q, zb, obank, of, ob = ({} for k in range(10))

        def chunk(name, c, tag=None):
            return sb("%s%d" % (name, c), [P, PACK, W], F32, tag)

        def power(c):
            pw[c] = chunk("pw", c, ("wa_q1", "wa_s1")[c] if c < 2 else None)
            cols = slice(c * W % HALF, c * W % HALF + W)
            if c * W < HALF:
                for u in range(2):
                    nc.scalar.activation(out=pw[c][:, 2 * u : 2 * u + 2, :], in_=abank[u][:, :, cols], func=ACT.Square)
            else:
                for t in range(PACK):
                    nc.scalar.activation(out=pw[c][:, t, :], in_=bbank[t][:, cols], func=ACT.Square)

        def gather(c):
            g[c] = chunk("g", c, "gg%d" % (c - 2) if c >= 2 else (None, "w1w")[c])
            for t in range(PACK):
                nc.vector.tensor_copy(g[c][:, t, :], y[t][:].indirect(fl_sb[:, c * W // 16 : (c + 1) * W // 16]))

        def square(c):
            gg[c] = chunk("gg", c, "root%d" % (c - 2) if c >= 2 else None)
            nc.scalar.activation(out=gg[c][:], in_=g[c][:], func=ACT.Square)

        def denominator(c):
            d = chunk("d", c)
            nc.vector.scalar_tensor_tensor(out=d[:], in0=gg[c][:], scalar=0.25, in1=pw[c][:], op0=ALU.add, op1=ALU.add)
            root[c] = chunk("root", c)
            nc.scalar.activation(out=root[c][:], in_=d[:], func=ACT.Abs_reciprocal_sqrt, scale=0.5)

        def inverse(c):
            r[c] = chunk("r", c)
            nc.scalar.activation(out=r[c][:], in_=root[c][:], func=ACT.Square)

        def share(c):
            q[c] = chunk("q", c)
            for t in range(PACK):
                nc.vector.scalar_tensor_tensor(
                    out=q[c][:, t, :], in0=pw[c][:, t, :], scalar=gt_sb[:, t : t + 1], in1=r[c][:, t, :], op0=ALU.mult, op1=ALU.mult
                )

        def make_z(c):
            zb[c] = sb("zb%d" % c, [P, W * PACK], BF16)
            nc.vector.tensor_tensor(out=woven(zb[c][:]), in0=planes(q[c][:]), in1=planes(g[c][:]), op=ALU.mult)

        def mix(c):
            zq = sb("zq%d" % c, [P, W], U32)
            zs = sb("zs%d" % c, [P, W], U8)
            quantise(zq[:], zs[:], zb[c][:])
            obank[c] = [psum.tile([P, 2, W], F32, name="obank%d%d" % (c, u), tag=bank_tags[2 * c + u]) for u in range(2)]
            for t in range(PACK):
                product(obank[c][t // 2][:, t % 2, :], d1w, d1s, t, zq[:], zs[:])

        def hand_out(c):
            cols = slice(c * W, (c + 1) * W)
            ob[c] = sb("ob%d" % c, [P, W * PACK], BF16)
            for u in range(2):
                nc.scalar.copy(out=of[c][:, 2 * u : 2 * u + 2, :], in_=obank[c][u][:])
            nc.sync.dma_start(out=out_rows[:, :, cols], in_=of[c])
            if c < ROUND_ON_SCALAR:
                nc.scalar.copy(out=woven(ob[c][:]), in_=planes(of[c]))
            else:
                nc.vector.tensor_copy(out=woven(ob[c][:]), in_=planes(of[c]))
            quantise(o_q[:, cols], o_s[:, cols], ob[c][:])
            if c >= n - 2:
                done = slice(0 if c == n - 2 else c * W, (c + 1) * W)
                nc.sync.dma_start(out=out_words[:, done], in_=o_q[:, done].bitcast(I32))

        for c in range(2):
            power(c)
            gather(c)
            square(c)
        for s in range(n + 2):
            if s < n:
                denominator(s)
            if 2 <= s + 1 < n:
                square(s + 1)
            if s + 2 < n:
                power(s + 2)
            if s < n:
                inverse(s)
            if 0 <= s - 2:
                make_z(s - 2)
            if s + 2 < n:
                gather(s + 2)
            if 0 <= s - 1 < n:
                share(s - 1)
            if 0 <= s - 2:
                mix(s - 2)
        early = sb("of_early", [P, 2, PACK, W], F32, "root%d" % (n - 1))
        for c in range(n):
            of[c] = early[:, c, :, :] if c < 2 else chunk("of", c)[:]
            hand_out(c)

        for row in range(4):
            queue = nc.sync if row % 2 == 0 else nc.scalar
            queue.dma_start(out=out_2[0, row:16:4, :].bitcast(I32), in_=o_s[row:P:32, :].bitcast(I32))
